import numpy as np
import ml_dtypes


def mxq(x, axis, fmt="e4m3"):
    dtype, down = {"e4m3": (ml_dtypes.float8_e4m3fn, 7), "e5m2": (ml_dtypes.float8_e5m2, 14)}[fmt]
    v = np.moveaxis(np.asarray(x, np.float32).astype(ml_dtypes.bfloat16).astype(np.float64), axis, -1)
    blocks = v.reshape(v.shape[:-1] + (-1, 32))
    amax = np.abs(blocks).max(-1, keepdims=True)
    byte = np.maximum(np.where(amax > 0, np.frexp(amax)[1] - 1 + 127, 0) - down, 1)
    scale = np.exp2(byte - 127.0)
    codes = (blocks / scale).astype(np.float32).astype(dtype).astype(np.float64)
    return np.moveaxis((codes * scale).reshape(v.shape), -1, axis)


WIDE = False


def mx_kscale(k):
    if not WIDE:
        return np.ones(k)
    levels = np.array([10, -10, 5, -5, 0])
    if k % 512:
        return np.exp2(np.random.permutation(np.resize(levels, k // 32))).repeat(32)
    a = np.empty((k // 512, 16))
    for p in range(k // 512):
        a[p, :8] = np.random.permutation(np.resize(levels, 8))
        for g in range(8):
            far = levels[np.abs(levels - a[p, g]) >= 10]
            a[p, g + 8] = far[np.random.randint(len(far))]
    return np.exp2(a.ravel()).repeat(32)


def f64(x):
    return np.asarray(x).astype(np.float64)


E2M1 = np.array([0.0, 0.5, 1.0, 1.5, 2.0, 3.0, 4.0, 6.0, -0.0, -0.5, -1.0, -1.5, -2.0, -3.0, -4.0, -6.0])


def pack_weight(w, fmt):
    k, n = w.shape
    w = f64(np.asarray(w, np.float32).astype(ml_dtypes.bfloat16)).reshape(k // 32, 32, n)
    amax = np.abs(w).max(1)
    if fmt == "e4m3":
        byte = np.frexp(amax)[1] - 1 + 127 - 7
    else:
        mant, ex = np.frexp(amax / 6.0)
        byte = np.where(mant > 0.5, ex, ex - 1) + 127
    byte = np.clip(np.where(amax > 0, byte, 1), 1, 254)
    scaled = (w * np.exp2(127.0 - byte)[:, None, :]).reshape(k, n).astype(np.float32)
    by_word = np.ascontiguousarray(scaled.reshape(k // 512, 128, 4, n).transpose(0, 1, 3, 2))
    if fmt == "e4m3":
        words = by_word.astype(ml_dtypes.float8_e4m3fn).view(np.uint8)
    else:
        c = by_word.astype(ml_dtypes.float4_e2m1fn).view(np.uint8) & 0xF
        words = (c[..., 0::2] | (c[..., 1::2] << 4)).reshape(k // 512, 128, 2 * n)
    return np.ascontiguousarray(words), np.ascontiguousarray(byte.astype(np.uint8).reshape(k // 512, 16, n))


def unpack_weight(words, scales, fmt):
    g, _, n = scales.shape
    words = np.ascontiguousarray(words).reshape(g, 128, n, -1)
    if fmt == "e4m3":
        vals = words.view(ml_dtypes.float8_e4m3fn).astype(np.float64)
    else:
        nib = np.empty((g, 128, n, 4), np.uint8)
        nib[..., 0::2] = words & 0xF
        nib[..., 1::2] = words >> 4
        vals = E2M1[nib]
    vals = vals * np.repeat(np.exp2(scales.astype(np.float64) - 127.0), 8, axis=1)[..., None]
    return vals.transpose(0, 1, 3, 2).reshape(g * 512, n)


K, L, T, R, N = 1024, 512, 512, 512, 512


def setup_inputs():
    n = np.random.standard_normal
    fk = mx_kscale(K)
    fr = mx_kscale(R)
    fl = mx_kscale(L)
    xtp = pack_weight(n((K, T)) / fk[:, None], "e4m3")
    wap = pack_weight(n((K, R)) * 1 / np.sqrt(K) * fk[:, None] * fr, "e2m1")
    cqp = pack_weight(n((L, T)) / fl[:, None], "e4m3")
    wcp = pack_weight(n((L, R)) * 1 / np.sqrt(L) * fl[:, None] * fr, "e2m1")
    wbp = pack_weight(n((R, N)) * 1 / np.sqrt(R) / fr[:, None], "e4m3")
    wyp = pack_weight(n((K, N)) * 1 / np.sqrt(K) * fk[:, None], "e2m1")
    return {
        "xt_words": xtp[0],
        "xt_scales": xtp[1],
        "wa_words": wap[0],
        "wa_scales": wap[1],
        "cq_words": cqp[0],
        "cq_scales": cqp[1],
        "wc_words": wcp[0],
        "wc_scales": wcp[1],
        "wb_words": wbp[0],
        "wb_scales": wbp[1],
        "wy_words": wyp[0],
        "wy_scales": wyp[1],
    }


def reference(xt_words, xt_scales, wa_words, wa_scales, cq_words, cq_scales, wc_words, wc_scales, wb_words, wb_scales, wy_words, wy_scales):
    xtu = unpack_weight(xt_words, xt_scales, "e4m3")
    wau = unpack_weight(wa_words, wa_scales, "e2m1")
    cqu = unpack_weight(cq_words, cq_scales, "e4m3")
    wcu = unpack_weight(wc_words, wc_scales, "e2m1")
    wbu = unpack_weight(wb_words, wb_scales, "e4m3")
    wyu = unpack_weight(wy_words, wy_scales, "e2m1")
    z = wau.T @ xtu + wcu.T @ cqu
    hid = np.maximum(z, 0.0)
    hidq = mxq(hid, 0, "e4m3")
    y = wbu.T @ hidq + wyu.T @ xtu
    return y

@@ -1,0 +1,186 @@
+from contextlib import ExitStack
+
+import concourse.mybir as mybir
+from concourse.masks import make_identity
+
+K, L, T, R, N = 1024, 512, 512, 512, 512
+FLOPS = 2 * (K * R * T + L * R * T + R * N * T + K * N * T)
+
+F32 = mybir.dt.float32
+BF16 = mybir.dt.bfloat16
+I32 = mybir.dt.int32
+U32 = mybir.dt.uint32
+U8 = mybir.dt.uint8
+FP8X4 = mybir.dt.float8_e4m3fn_x4
+FP4X4 = mybir.dt.float4_e2m1fn_x4
+
+P = 128
+WIDTH = 512
+TILES = WIDTH // P
+HALF = WIDTH // 2
+ROWS = 4
+
+
+def cols(i, width=P):
+    return slice(i * width, (i + 1) * width)
+
+
+def tile_mix_conditioned_hidden_kernel(
+    tc, xt_words, xt_scales, wa_words, wa_scales, cq_words, cq_scales,
+    wc_words, wc_scales, wb_words, wb_scales, wy_words, wy_scales, out,
+):
+    nc = tc.nc
+    with ExitStack() as ctx:
+        keep = ctx.enter_context(tc.tile_pool(name="keep", bufs=1))
+        psum = ctx.enter_context(tc.psum_pool(name="psum", bufs=1))
+        ctx.enter_context(tc.manual_schedule())
+
+        def fp8_tile(name, passes):
+            return keep.tile([P, passes, WIDTH], U32, name=name, align_bytes=64)
+
+        def byte_tile(name, passes, width):
+            return keep.tile([P, passes, width], U8, name=name, align_bytes=64)
+
+        xt, cq, wb = fp8_tile("xt", 2), fp8_tile("cq", 1), fp8_tile("wb", 1)
+        wa, wc, wy = byte_tile("wa", 2, 2 * WIDTH), byte_tile("wc", 1, 2 * WIDTH), byte_tile("wy", 2, 2 * WIDTH)
+        xt_s, cq_s, wb_s = byte_tile("xt_s", 2, WIDTH), byte_tile("cq_s", 1, WIDTH), byte_tile("wb_s", 1, WIDTH)
+        wa_s, wc_s, wy_s = byte_tile("wa_s", 2, WIDTH), byte_tile("wc_s", 1, WIDTH), byte_tile("wy_s", 2, WIDTH)
+
+        for plane in (wa_s, xt_s, cq_s, wc_s, wy_s, wb_s):
+            nc.vector.memset(plane[:].bitcast(U32), 0)
+        identity = keep.tile([P, P], F32, name="identity")
+        nc.vector.memset(identity[:], 0.0)
+        make_identity(nc, identity[:], nomemset=True)
+
+        def load_fp8(queue, tile, words):
+            queue.dma_start(out=tile[:].bitcast(I32), in_=words.rearrange("z p c t -> p z (c t)").bitcast(I32))
+
+        def load_fp4(queue, tile, words):
+            queue.dma_start(out=tile[:].bitcast(I32), in_=words.rearrange("z p c -> p z c").bitcast(I32))
+
+        def load_scale_row(queue, plane, scales, r):
+            queue.dma_start(
+                out=plane[:].bitcast(I32)[r:P:32, :, :],
+                in_=scales.bitcast(I32)[:, r:16:ROWS, :].rearrange("z q c -> q z c"),
+            )
+
+        load_fp4(nc.sync, wa, wa_words)
+        load_scale_row(nc.sync, wa_s, wa_scales, 0)
+        load_fp8(nc.sync, xt, xt_words)
+        load_scale_row(nc.scalar, wa_s, wa_scales, 1)
+        load_scale_row(nc.scalar, wa_s, wa_scales, 2)
+        load_scale_row(nc.sync, wa_s, wa_scales, 3)
+        load_scale_row(nc.scalar, xt_s, xt_scales, 0)
+        load_scale_row(nc.sync, xt_s, xt_scales, 1)
+        load_scale_row(nc.scalar, xt_s, xt_scales, 2)
+        load_scale_row(nc.scalar, xt_s, xt_scales, 3)
+        for r in range(ROWS):
+            load_scale_row(nc.sync, cq_s, cq_scales, r)
+        for r in range(ROWS):
+            load_scale_row(nc.sync, wc_s, wc_scales, r)
+        load_fp8(nc.sync, cq, cq_words)
+        load_fp4(nc.sync, wc, wc_words)
+        for r in range(ROWS):
+            load_scale_row(nc.sync, wy_s, wy_scales, r)
+        load_fp4(nc.sync, wy, wy_words)
+        for r in range(ROWS):
+            load_scale_row(nc.sync, wb_s, wb_scales, r)
+        load_fp8(nc.sync, wb, wb_words)
+
+        z = [psum.tile([P, WIDTH], F32, name="z%d" % i, tag="z%d" % i) for i in range(TILES)]
+        hid_t = [keep.tile([P, WIDTH], BF16, name="hid_t%d" % i, align_bytes=64) for i in range(TILES)]
+        grouped = [keep.tile([P, HALF * 4], BF16, name="grouped%d" % h, align_bytes=64) for h in range(2)]
+        hid = keep.tile([P, WIDTH], U32, name="hid", align_bytes=64)
+        hid_s = keep.tile([P, WIDTH], U8, name="hid_s", align_bytes=64)
+
+        def token_product(i):
+            for g in range(2):
+                nc.tensor.matmul_mx(
+                    out=z[i][:], lhsT=xt[:, g, cols(i)].bitcast(FP8X4), lhsT_scale=xt_s[:, g, cols(i)],
+                    rhs=wa[:, g, :].bitcast(FP4X4), rhs_scale=wa_s[:, g, :], start=(g == 0), stop=False,
+                )
+
+        def condition_product(i):
+            nc.tensor.matmul_mx(
+                out=z[i][:], lhsT=cq[:, 0, cols(i)].bitcast(FP8X4), lhsT_scale=cq_s[:, 0, cols(i)],
+                rhs=wc[:, 0, :].bitcast(FP4X4), rhs_scale=wc_s[:, 0, :], start=False, stop=True,
+            )
+
+        def relu(i):
+            src = z[i][:].rearrange("t (p u e) -> t u p e", u=2, e=2)
+            dst = hid_t[i][:].rearrange("t (u p e) -> t u p e", u=2, e=2)
+            if i % 2 == 0:
+                nc.vector.tensor_scalar(out=dst, in0=src, scalar1=0.0, scalar2=None, op0=mybir.AluOpType.max)
+            else:
+                nc.scalar.activation(out=dst, in_=src, func=mybir.ActivationFunctionType.Relu)
+
+        for i in range(TILES - 1):
+            token_product(i)
+        for i in range(TILES - 1):
+            condition_product(i)
+            relu(i)
+        token_product(TILES - 1)
+        condition_product(TILES - 1)
+        relu(TILES - 1)
+
+        turned = []
+        for i in range(TILES):
+            bank = psum.tile([P, 2, P], F32, name="turned%d" % i, tag="z%d" % i)
+            turned.append(bank)
+            for u in range(2):
+                nc.tensor.transpose(bank[:, u, :], hid_t[i][:].bitcast(F32)[:, cols(u)], identity[:])
+
+        def interleave(i):
+            dst = grouped[i // 2][:].bitcast(F32)[:, cols(i % 2, 2 * P)].rearrange("p (t u) -> p t u", u=2)
+            src = turned[i][:].rearrange("p u t -> p t u")
+            if i % 2 == 0:
+                nc.vector.tensor_copy(out=dst, in_=src)
+            else:
+                nc.scalar.copy(out=dst, in_=src)
+
+        def quantise(h):
+            nc.vector.quantize_mx(out=hid[:, cols(h, HALF)].bitcast(FP8X4), scales=hid_s[:, cols(h, HALF)], in_=grouped[h][:])
+
+        for i in range(TILES):
+            interleave(i)
+        quantise(0)
+        quantise(1)
+
+        y = [psum.tile([P, WIDTH], F32, name="y%d" % c, tag="y%d" % c) for c in range(TILES)]
+        result = [keep.tile([P, WIDTH], F32, name="result%d" % c) for c in range(TILES)]
+
+        def skip_product(c):
+            for g in range(2):
+                nc.tensor.matmul_mx(
+                    out=y[c][:], lhsT=wy[:, g, cols(c, 2 * P)].bitcast(FP4X4), lhsT_scale=wy_s[:, g, cols(c)],
+                    rhs=xt[:, g, :].bitcast(FP8X4), rhs_scale=xt_s[:, g, :], start=(g == 0), stop=False,
+                )
+
+        def hidden_product(c):
+            nc.tensor.matmul_mx(
+                out=y[c][:], lhsT=wb[:, 0, cols(c)].bitcast(FP8X4), lhsT_scale=wb_s[:, 0, cols(c)],
+                rhs=hid[:].bitcast(FP8X4), rhs_scale=hid_s[:], start=False, stop=True,
+            )
+
+        def store(c, pieces):
+            width = WIDTH // pieces
+            for piece in range(pieces):
+                part = cols(piece, width)
+                if c % 2 == 0:
+                    nc.scalar.copy(out=result[c][:, part], in_=y[c][:, part])
+                else:
+                    nc.vector.tensor_copy(out=result[c][:, part], in_=y[c][:, part])
+                nc.sync.dma_start(out=out[cols(c), part], in_=result[c][:, part])
+
+        skip_product(0)
+        skip_product(1)
+        hidden_product(0)
+        store(0, 1)
+        hidden_product(1)
+        store(1, 1)
+        skip_product(2)
+        hidden_product(2)
+        store(2, 1)
+        skip_product(3)
+        hidden_product(3)
+        store(3, 2)

@@ -1,7 +1,6 @@
 from contextlib import ExitStack
 
 import concourse.mybir as mybir
-from concourse.masks import make_identity
 
 K, L, T, R, N = 1024, 512, 512, 512, 512
 FLOPS = 2 * (K * R * T + L * R * T + R * N * T + K * N * T)
@@ -19,6 +18,7 @@ WIDTH = 512
 TILES = WIDTH // P
 HALF = WIDTH // 2
 ROWS = 4
+WARM_UP = 8
 
 
 def cols(i, width=P):
@@ -41,16 +41,14 @@ def tile_mix_conditioned_hidden_kernel(
         def byte_tile(name, passes, width):
             return keep.tile([P, passes, width], U8, name=name, align_bytes=64)
 
-        xt, cq, wb = fp8_tile("xt", 2), fp8_tile("cq", 1), fp8_tile("wb", 1)
+        xt = [fp8_tile("xt%d" % g, 1) for g in range(2)]
+        cq, wb = fp8_tile("cq", 1), fp8_tile("wb", 1)
         wa, wc, wy = byte_tile("wa", 2, 2 * WIDTH), byte_tile("wc", 1, 2 * WIDTH), byte_tile("wy", 2, 2 * WIDTH)
         xt_s, cq_s, wb_s = byte_tile("xt_s", 2, WIDTH), byte_tile("cq_s", 1, WIDTH), byte_tile("wb_s", 1, WIDTH)
         wa_s, wc_s, wy_s = byte_tile("wa_s", 2, WIDTH), byte_tile("wc_s", 1, WIDTH), byte_tile("wy_s", 2, WIDTH)
 
-        for plane in (wa_s, xt_s, cq_s, wc_s, wy_s, wb_s):
+        for plane in (wa_s, xt_s, wy_s, wc_s, cq_s, wb_s):
             nc.vector.memset(plane[:].bitcast(U32), 0)
-        identity = keep.tile([P, P], F32, name="identity")
-        nc.vector.memset(identity[:], 0.0)
-        make_identity(nc, identity[:], nomemset=True)
 
         def load_fp8(queue, tile, words):
             queue.dma_start(out=tile[:].bitcast(I32), in_=words.rearrange("z p c t -> p z (c t)").bitcast(I32))
@@ -64,102 +62,113 @@ def tile_mix_conditioned_hidden_kernel(
                 in_=scales.bitcast(I32)[:, r:16:ROWS, :].rearrange("z q c -> q z c"),
             )
 
-        load_fp4(nc.sync, wa, wa_words)
+        load_fp8(nc.sync, xt[0], xt_words[0:1])
         load_scale_row(nc.sync, wa_s, wa_scales, 0)
-        load_fp8(nc.sync, xt, xt_words)
         load_scale_row(nc.scalar, wa_s, wa_scales, 1)
-        load_scale_row(nc.scalar, wa_s, wa_scales, 2)
-        load_scale_row(nc.sync, wa_s, wa_scales, 3)
-        load_scale_row(nc.scalar, xt_s, xt_scales, 0)
-        load_scale_row(nc.sync, xt_s, xt_scales, 1)
-        load_scale_row(nc.scalar, xt_s, xt_scales, 2)
-        load_scale_row(nc.scalar, xt_s, xt_scales, 3)
+        load_scale_row(nc.sync, wa_s, wa_scales, 2)
+        load_scale_row(nc.scalar, wa_s, wa_scales, 3)
+        load_fp4(nc.sync, wa, wa_words)
+        for r in range(ROWS):
+            load_scale_row(nc.scalar if r < 2 else nc.sync, xt_s, xt_scales, r)
+        for r in range(ROWS - 1):
+            load_scale_row(nc.sync, wc_s, wc_scales, r)
+        load_fp8(nc.sync, xt[1], xt_words[1:2])
+        load_scale_row(nc.sync, wc_s, wc_scales, ROWS - 1)
+        load_fp4(nc.sync, wc, wc_words)
+        load_fp8(nc.sync, cq, cq_words)
         for r in range(ROWS):
             load_scale_row(nc.sync, cq_s, cq_scales, r)
-        for r in range(ROWS):
-            load_scale_row(nc.sync, wc_s, wc_scales, r)
-        load_fp8(nc.sync, cq, cq_words)
-        load_fp4(nc.sync, wc, wc_words)
-        for r in range(ROWS):
-            load_scale_row(nc.sync, wy_s, wy_scales, r)
         load_fp4(nc.sync, wy, wy_words)
         for r in range(ROWS):
-            load_scale_row(nc.sync, wb_s, wb_scales, r)
+            load_scale_row(nc.gpsimd if r < 2 else nc.sync, wy_s, wy_scales, r)
         load_fp8(nc.sync, wb, wb_words)
+        for r in range(ROWS):
+            load_scale_row(nc.sync, wb_s, wb_scales, r)
 
-        z = [psum.tile([P, WIDTH], F32, name="z%d" % i, tag="z%d" % i) for i in range(TILES)]
-        hid_t = [keep.tile([P, WIDTH], BF16, name="hid_t%d" % i, align_bytes=64) for i in range(TILES)]
-        grouped = [keep.tile([P, HALF * 4], BF16, name="grouped%d" % h, align_bytes=64) for h in range(2)]
+        def sort_codes(name, words, g):
+            codes = keep.tile([P, 2 * WIDTH], U8, name=name, align_bytes=64)
+            nc.vector.tensor_copy(
+                out=codes[:].rearrange("p (j m b) -> p j m b", j=4, b=2),
+                in_=words[:, g, :].rearrange("p (m j b) -> p j m b", j=4, b=2),
+            )
+            return codes
+
+        def sort_scales(name, plane, g):
+            scales = keep.tile([P, WIDTH], U8, name=name, align_bytes=64)
+            nc.vector.tensor_copy(
+                out=scales[:].rearrange("p (j m) -> p j m", j=4),
+                in_=plane[:, g, :].rearrange("p (m j) -> p j m", j=4),
+            )
+            return scales
+
+        wa_sorted_s = [sort_scales("wa_sorted_s%d" % g, wa_s, g) for g in range(2)]
+        wa_sorted = [(sort_codes("wa_sorted%d" % g, wa, g), wa_sorted_s[g]) for g in range(2)]
+        wc_sorted_s = sort_scales("wc_sorted_s", wc_s, 0)
+        wc_sorted = (sort_codes("wc_sorted", wc, 0), wc_sorted_s)
+
+        y = [psum.tile([P, WIDTH], F32, name="y%d" % c, tag="y%d" % c) for c in range(TILES)]
+        for w in range(WARM_UP):
+            nc.tensor.matmul_mx(
+                out=y[TILES - 1][:, cols(0)], lhsT=xt[0][:, 0, cols(0)].bitcast(FP8X4), lhsT_scale=wa_s[:, 0, cols(0)],
+                rhs=xt[0][:, 0, cols(1)].bitcast(FP8X4), rhs_scale=wa_s[:, 0, cols(1)], start=True, stop=True,
+            )
+
+        z = [psum.tile([P, 4, P], F32, name="z%d" % i, tag="z%d" % i) for i in range(TILES)]
+        grouped = [keep.tile([P, WIDTH], BF16, name="grouped%d" % i, align_bytes=64) for i in range(TILES)]
         hid = keep.tile([P, WIDTH], U32, name="hid", align_bytes=64)
         hid_s = keep.tile([P, WIDTH], U8, name="hid_s", align_bytes=64)
 
-        def token_product(i):
-            for g in range(2):
+        def first_layer_pass(i, weights, codes, scales, first, last):
+            for j in range(4):
                 nc.tensor.matmul_mx(
-                    out=z[i][:], lhsT=xt[:, g, cols(i)].bitcast(FP8X4), lhsT_scale=xt_s[:, g, cols(i)],
-                    rhs=wa[:, g, :].bitcast(FP4X4), rhs_scale=wa_s[:, g, :], start=(g == 0), stop=False,
+                    out=z[i][:, j, :], lhsT=weights[0][:, cols(j, 2 * P)].bitcast(FP4X4), lhsT_scale=weights[1][:, cols(j)],
+                    rhs=codes.bitcast(FP8X4), rhs_scale=scales, start=(first and j == 0), stop=(last and j == 3),
                 )
 
+        def token_product(i, g):
+            first_layer_pass(i, wa_sorted[g], xt[g][:, 0, cols(i)], xt_s[:, g, cols(i)], g == 0, False)
+
         def condition_product(i):
-            nc.tensor.matmul_mx(
-                out=z[i][:], lhsT=cq[:, 0, cols(i)].bitcast(FP8X4), lhsT_scale=cq_s[:, 0, cols(i)],
-                rhs=wc[:, 0, :].bitcast(FP4X4), rhs_scale=wc_s[:, 0, :], start=False, stop=True,
-            )
+            first_layer_pass(i, wc_sorted, cq[:, 0, cols(i)], cq_s[:, 0, cols(i)], False, True)
 
         def relu(i):
-            src = z[i][:].rearrange("t (p u e) -> t u p e", u=2, e=2)
-            dst = hid_t[i][:].rearrange("t (u p e) -> t u p e", u=2, e=2)
-            if i % 2 == 0:
+            src = z[i][:].rearrange("p j t -> p t j")
+            dst = grouped[i][:].rearrange("p (t j) -> p t j", j=4)
+            if i == 1:
                 nc.vector.tensor_scalar(out=dst, in0=src, scalar1=0.0, scalar2=None, op0=mybir.AluOpType.max)
             else:
                 nc.scalar.activation(out=dst, in_=src, func=mybir.ActivationFunctionType.Relu)
 
+        def quantise(i):
+            nc.vector.quantize_mx(out=hid[:, cols(i)].bitcast(FP8X4), scales=hid_s[:, cols(i)], in_=grouped[i][:])
+
+        for i in range(TILES):
+            token_product(i, 0)
         for i in range(TILES - 1):
-            token_product(i)
+            token_product(i, 1)
         for i in range(TILES - 1):
             condition_product(i)
             relu(i)
-        token_product(TILES - 1)
+        token_product(TILES - 1, 1)
         condition_product(TILES - 1)
         relu(TILES - 1)
-
-        turned = []
         for i in range(TILES):
-            bank = psum.tile([P, 2, P], F32, name="turned%d" % i, tag="z%d" % i)
-            turned.append(bank)
-            for u in range(2):
-                nc.tensor.transpose(bank[:, u, :], hid_t[i][:].bitcast(F32)[:, cols(u)], identity[:])
+            quantise(i)
 
-        def interleave(i):
-            dst = grouped[i // 2][:].bitcast(F32)[:, cols(i % 2, 2 * P)].rearrange("p (t u) -> p t u", u=2)
-            src = turned[i][:].rearrange("p u t -> p t u")
-            if i % 2 == 0:
-                nc.vector.tensor_copy(out=dst, in_=src)
-            else:
-                nc.scalar.copy(out=dst, in_=src)
-
-        def quantise(h):
-            nc.vector.quantize_mx(out=hid[:, cols(h, HALF)].bitcast(FP8X4), scales=hid_s[:, cols(h, HALF)], in_=grouped[h][:])
-
-        for i in range(TILES):
-            interleave(i)
-        quantise(0)
-        quantise(1)
-
-        y = [psum.tile([P, WIDTH], F32, name="y%d" % c, tag="y%d" % c) for c in range(TILES)]
         result = [keep.tile([P, WIDTH], F32, name="result%d" % c) for c in range(TILES)]
 
         def skip_product(c):
             for g in range(2):
                 nc.tensor.matmul_mx(
                     out=y[c][:], lhsT=wy[:, g, cols(c, 2 * P)].bitcast(FP4X4), lhsT_scale=wy_s[:, g, cols(c)],
-                    rhs=xt[:, g, :].bitcast(FP8X4), rhs_scale=xt_s[:, g, :], start=(g == 0), stop=False,
+                    rhs=xt[g][:, 0, :].bitcast(FP8X4), rhs_scale=xt_s[:, g, :], start=(g == 0), stop=False,
                 )
 
-        def hidden_product(c):
+        def hidden_product(c, first=0, last=WIDTH):
+            part = slice(first, last)
             nc.tensor.matmul_mx(
-                out=y[c][:], lhsT=wb[:, 0, cols(c)].bitcast(FP8X4), lhsT_scale=wb_s[:, 0, cols(c)],
-                rhs=hid[:].bitcast(FP8X4), rhs_scale=hid_s[:], start=False, stop=True,
+                out=y[c][:, part], lhsT=wb[:, 0, cols(c)].bitcast(FP8X4), lhsT_scale=wb_s[:, 0, cols(c)],
+                rhs=hid[:, part].bitcast(FP8X4), rhs_scale=hid_s[:, part], start=False, stop=(last == WIDTH),
             )
 
         def store(c, pieces):
@@ -174,13 +183,16 @@ def tile_mix_conditioned_hidden_kernel(
 
         skip_product(0)
         skip_product(1)
-        hidden_product(0)
-        store(0, 1)
-        hidden_product(1)
-        store(1, 1)
+        for c in range(2):
+            hidden_product(c, 0, 2 * P)
+        for c in range(2):
+            hidden_product(c, 2 * P, 3 * P)
+        for c in range(2):
+            hidden_product(c, 3 * P, WIDTH)
+            store(c, 2)
         skip_product(2)
         hidden_product(2)
-        store(2, 1)
+        store(2, 2)
         skip_product(3)
         hidden_product(3)
         store(3, 2)

@@ -14,9 +14,12 @@ FP8X4 = mybir.dt.float8_e4m3fn_x4
 FP4X4 = mybir.dt.float4_e2m1fn_x4
 
 P = 128
+PACK = 4
 WIDTH = 512
 TILES = WIDTH // P
+LAST = TILES - 1
 HALF = WIDTH // 2
+QUADRANT = 32
 ROWS = 4
 WARM_UP = 8
 
@@ -35,164 +38,154 @@ def tile_mix_conditioned_hidden_kernel(
         psum = ctx.enter_context(tc.psum_pool(name="psum", bufs=1))
         ctx.enter_context(tc.manual_schedule())
 
-        def fp8_tile(name, passes):
-            return keep.tile([P, passes, WIDTH], U32, name=name, align_bytes=64)
+        def sbuf(name, shape, dtype):
+            return keep.tile(shape, dtype, name=name, align_bytes=64)
 
-        def byte_tile(name, passes, width):
-            return keep.tile([P, passes, width], U8, name=name, align_bytes=64)
-
-        xt = [fp8_tile("xt%d" % g, 1) for g in range(2)]
-        cq, wb = fp8_tile("cq", 1), fp8_tile("wb", 1)
-        wa, wc, wy = byte_tile("wa", 2, 2 * WIDTH), byte_tile("wc", 1, 2 * WIDTH), byte_tile("wy", 2, 2 * WIDTH)
-        xt_s, cq_s, wb_s = byte_tile("xt_s", 2, WIDTH), byte_tile("cq_s", 1, WIDTH), byte_tile("wb_s", 1, WIDTH)
-        wa_s, wc_s, wy_s = byte_tile("wa_s", 2, WIDTH), byte_tile("wc_s", 1, WIDTH), byte_tile("wy_s", 2, WIDTH)
+        xt = [sbuf("xt%d" % g, [P, 1, WIDTH], U32) for g in range(2)]
+        cq, wb = sbuf("cq", [P, 1, WIDTH], U32), sbuf("wb", [P, 1, WIDTH], U32)
+        wa, wc, wy = sbuf("wa", [P, 2, 2 * WIDTH], U8), sbuf("wc", [P, 1, 2 * WIDTH], U8), sbuf("wy", [P, 2, 2 * WIDTH], U8)
+        xt_s, cq_s, wb_s = sbuf("xt_s", [P, 2, WIDTH], U8), sbuf("cq_s", [P, 1, WIDTH], U8), sbuf("wb_s", [P, 1, WIDTH], U8)
+        wa_s, wc_s, wy_s = sbuf("wa_s", [P, 2, WIDTH], U8), sbuf("wc_s", [P, 1, WIDTH], U8), sbuf("wy_s", [P, 2, WIDTH], U8)
 
         for plane in (wa_s, xt_s, wy_s, wc_s, cq_s, wb_s):
             nc.vector.memset(plane[:].bitcast(U32), 0)
 
-        def load_fp8(queue, tile, words):
-            queue.dma_start(out=tile[:].bitcast(I32), in_=words.rearrange("z p c t -> p z (c t)").bitcast(I32))
+        def load_fp8(tile, words):
+            nc.sync.dma_start(out=tile[:].bitcast(I32), in_=words.rearrange("z p c t -> p z (c t)").bitcast(I32))
 
-        def load_fp4(queue, tile, words):
-            queue.dma_start(out=tile[:].bitcast(I32), in_=words.rearrange("z p c -> p z c").bitcast(I32))
+        def load_fp4(tile, words):
+            nc.sync.dma_start(out=tile[:].bitcast(I32), in_=words.rearrange("z p c -> p z c").bitcast(I32))
 
-        def load_scale_row(queue, plane, scales, r):
-            queue.dma_start(
-                out=plane[:].bitcast(I32)[r:P:32, :, :],
-                in_=scales.bitcast(I32)[:, r:16:ROWS, :].rearrange("z q c -> q z c"),
-            )
+        def load_scale_rows(queue, plane, scales, rows):
+            for r in rows:
+                queue.dma_start(
+                    out=plane[:].bitcast(I32)[r:P:QUADRANT, :, :],
+                    in_=scales.bitcast(I32)[:, r : 4 * ROWS : ROWS, :].rearrange("z q c -> q z c"),
+                )
 
-        load_fp8(nc.sync, xt[0], xt_words[0:1])
-        load_scale_row(nc.sync, wa_s, wa_scales, 0)
-        load_scale_row(nc.scalar, wa_s, wa_scales, 1)
-        load_scale_row(nc.sync, wa_s, wa_scales, 2)
-        load_scale_row(nc.scalar, wa_s, wa_scales, 3)
-        load_fp4(nc.sync, wa, wa_words)
-        for r in range(ROWS):
-            load_scale_row(nc.scalar if r < 2 else nc.sync, xt_s, xt_scales, r)
-        for r in range(ROWS - 1):
-            load_scale_row(nc.sync, wc_s, wc_scales, r)
-        load_fp8(nc.sync, xt[1], xt_words[1:2])
-        load_scale_row(nc.sync, wc_s, wc_scales, ROWS - 1)
-        load_fp4(nc.sync, wc, wc_words)
-        load_fp8(nc.sync, cq, cq_words)
-        for r in range(ROWS):
-            load_scale_row(nc.sync, cq_s, cq_scales, r)
-        load_fp4(nc.sync, wy, wy_words)
-        for r in range(ROWS):
-            load_scale_row(nc.gpsimd if r < 2 else nc.sync, wy_s, wy_scales, r)
-        load_fp8(nc.sync, wb, wb_words)
-        for r in range(ROWS):
-            load_scale_row(nc.sync, wb_s, wb_scales, r)
+        load_fp8(xt[0], xt_words[0:1])
+        load_scale_rows(nc.sync, wa_s, wa_scales, (0, 2))
+        load_scale_rows(nc.scalar, wa_s, wa_scales, (1, 3))
+        load_fp4(wa, wa_words)
+        load_scale_rows(nc.scalar, xt_s, xt_scales, (0, 1))
+        load_scale_rows(nc.sync, xt_s, xt_scales, (2, 3))
+        load_fp4(wc, wc_words)
+        load_scale_rows(nc.sync, wc_s, wc_scales, (0, 1))
+        load_fp8(xt[1], xt_words[1:2])
+        load_scale_rows(nc.sync, wc_s, wc_scales, (2, 3))
+        load_fp8(cq, cq_words)
+        load_scale_rows(nc.sync, cq_s, cq_scales, range(ROWS))
+        load_fp4(wy, wy_words)
+        load_scale_rows(nc.gpsimd, wy_s, wy_scales, (0, 1))
+        load_scale_rows(nc.sync, wy_s, wy_scales, (2, 3))
+        load_fp8(wb, wb_words)
+        load_scale_rows(nc.sync, wb_s, wb_scales, range(ROWS))
 
-        def sort_codes(name, words, g):
-            codes = keep.tile([P, 2 * WIDTH], U8, name=name, align_bytes=64)
-            nc.vector.tensor_copy(
-                out=codes[:].rearrange("p (j m b) -> p j m b", j=4, b=2),
-                in_=words[:, g, :].rearrange("p (m j b) -> p j m b", j=4, b=2),
-            )
-            return codes
+        def sort_scales(name, plane):
+            scales = sbuf(name, [P, PACK, P], U8)
+            nc.vector.tensor_copy(out=scales[:], in_=plane.rearrange("p (m j) -> p j m", j=PACK))
+            return [scales[:, j, :] for j in range(PACK)]
 
-        def sort_scales(name, plane, g):
-            scales = keep.tile([P, WIDTH], U8, name=name, align_bytes=64)
-            nc.vector.tensor_copy(
-                out=scales[:].rearrange("p (j m) -> p j m", j=4),
-                in_=plane[:, g, :].rearrange("p (m j) -> p j m", j=4),
-            )
-            return scales
+        def sort_codes(name, words, pieces):
+            by_slot = words.rearrange("p (m j b) -> p j m b", j=PACK, b=2)
+            per_piece = PACK // pieces
+            result = []
+            for piece in range(pieces):
+                codes = sbuf("%s_%d" % (name, piece), [P, per_piece * 2 * P], U8)
+                nc.vector.tensor_copy(
+                    out=codes[:].rearrange("p (j m b) -> p j m b", j=per_piece, b=2),
+                    in_=by_slot[:, cols(piece, per_piece), :, :],
+                )
+                result.extend(codes[:, cols(j, 2 * P)] for j in range(per_piece))
+            return result
 
-        wa_sorted_s = [sort_scales("wa_sorted_s%d" % g, wa_s, g) for g in range(2)]
-        wa_sorted = [(sort_codes("wa_sorted%d" % g, wa, g), wa_sorted_s[g]) for g in range(2)]
-        wc_sorted_s = sort_scales("wc_sorted_s", wc_s, 0)
-        wc_sorted = (sort_codes("wc_sorted", wc, 0), wc_sorted_s)
+        wa_sorted_s = [sort_scales("wa_sorted_s%d" % g, wa_s[:, g, :]) for g in range(2)]
+        wa_sorted = [sort_codes("wa_sorted0", wa[:, 0, :], PACK), sort_codes("wa_sorted1", wa[:, 1, :], 1)]
+        wc_sorted = sort_codes("wc_sorted", wc[:, 0, :], 1)
+        wc_sorted_s = sort_scales("wc_sorted_s", wc_s[:, 0, :])
 
         y = [psum.tile([P, WIDTH], F32, name="y%d" % c, tag="y%d" % c) for c in range(TILES)]
         for w in range(WARM_UP):
             nc.tensor.matmul_mx(
-                out=y[TILES - 1][:, cols(0)], lhsT=xt[0][:, 0, cols(0)].bitcast(FP8X4), lhsT_scale=wa_s[:, 0, cols(0)],
+                out=y[LAST][:, cols(0)], lhsT=xt[0][:, 0, cols(0)].bitcast(FP8X4), lhsT_scale=wa_s[:, 0, cols(0)],
                 rhs=xt[0][:, 0, cols(1)].bitcast(FP8X4), rhs_scale=wa_s[:, 0, cols(1)], start=True, stop=True,
             )
 
-        z = [psum.tile([P, 4, P], F32, name="z%d" % i, tag="z%d" % i) for i in range(TILES)]
-        grouped = [keep.tile([P, WIDTH], BF16, name="grouped%d" % i, align_bytes=64) for i in range(TILES)]
-        hid = keep.tile([P, WIDTH], U32, name="hid", align_bytes=64)
-        hid_s = keep.tile([P, WIDTH], U8, name="hid_s", align_bytes=64)
+        z = [psum.tile([P, PACK, P], F32, name="z%d" % i, tag="z%d" % i) for i in range(TILES)]
+        grouped = [sbuf("grouped%d" % i, [P, P * PACK], BF16) for i in range(TILES)]
+        hid = sbuf("hid", [P, WIDTH], U32)
+        hid_s = sbuf("hid_s", [P, WIDTH], U8)
 
-        def first_layer_pass(i, weights, codes, scales, first, last):
-            for j in range(4):
-                nc.tensor.matmul_mx(
-                    out=z[i][:, j, :], lhsT=weights[0][:, cols(j, 2 * P)].bitcast(FP4X4), lhsT_scale=weights[1][:, cols(j)],
-                    rhs=codes.bitcast(FP8X4), rhs_scale=scales, start=(first and j == 0), stop=(last and j == 3),
-                )
+        def token_pass(i, g, j):
+            nc.tensor.matmul_mx(
+                out=z[i][:, j, :], lhsT=wa_sorted[g][j].bitcast(FP4X4), lhsT_scale=wa_sorted_s[g][j],
+                rhs=xt[g][:, 0, cols(i)].bitcast(FP8X4), rhs_scale=xt_s[:, g, cols(i)],
+                start=(g == 0 and j == 0), stop=False,
+            )
 
-        def token_product(i, g):
-            first_layer_pass(i, wa_sorted[g], xt[g][:, 0, cols(i)], xt_s[:, g, cols(i)], g == 0, False)
+        def condition_pass(i, j):
+            nc.tensor.matmul_mx(
+                out=z[i][:, j, :], lhsT=wc_sorted[j].bitcast(FP4X4), lhsT_scale=wc_sorted_s[j],
+                rhs=cq[:, 0, cols(i)].bitcast(FP8X4), rhs_scale=cq_s[:, 0, cols(i)],
+                start=False, stop=(j == PACK - 1),
+            )
 
-        def condition_product(i):
-            first_layer_pass(i, wc_sorted, cq[:, 0, cols(i)], cq_s[:, 0, cols(i)], False, True)
-
-        def relu(i):
+        def close_tile(i):
+            for j in range(PACK):
+                condition_pass(i, j)
             src = z[i][:].rearrange("p j t -> p t j")
-            dst = grouped[i][:].rearrange("p (t j) -> p t j", j=4)
+            dst = grouped[i][:].rearrange("p (t j) -> p t j", j=PACK)
             if i == 1:
                 nc.vector.tensor_scalar(out=dst, in0=src, scalar1=0.0, scalar2=None, op0=mybir.AluOpType.max)
             else:
                 nc.scalar.activation(out=dst, in_=src, func=mybir.ActivationFunctionType.Relu)
 
-        def quantise(i):
+        for j in range(PACK):
+            for i in range(TILES):
+                token_pass(i, 0, j)
+        for i in range(LAST):
+            for j in range(PACK):
+                token_pass(i, 1, j)
+        for i in range(LAST):
+            close_tile(i)
+        for j in range(PACK):
+            token_pass(LAST, 1, j)
+        close_tile(LAST)
+        for i in range(TILES):
             nc.vector.quantize_mx(out=hid[:, cols(i)].bitcast(FP8X4), scales=hid_s[:, cols(i)], in_=grouped[i][:])
-
-        for i in range(TILES):
-            token_product(i, 0)
-        for i in range(TILES - 1):
-            token_product(i, 1)
-        for i in range(TILES - 1):
-            condition_product(i)
-            relu(i)
-        token_product(TILES - 1, 1)
-        condition_product(TILES - 1)
-        relu(TILES - 1)
-        for i in range(TILES):
-            quantise(i)
 
         result = [keep.tile([P, WIDTH], F32, name="result%d" % c) for c in range(TILES)]
 
-        def skip_product(c):
+        def skip_product(bank, c):
             for g in range(2):
                 nc.tensor.matmul_mx(
-                    out=y[c][:], lhsT=wy[:, g, cols(c, 2 * P)].bitcast(FP4X4), lhsT_scale=wy_s[:, g, cols(c)],
+                    out=bank[:], lhsT=wy[:, g, cols(c, 2 * P)].bitcast(FP4X4), lhsT_scale=wy_s[:, g, cols(c)],
                     rhs=xt[g][:, 0, :].bitcast(FP8X4), rhs_scale=xt_s[:, g, :], start=(g == 0), stop=False,
                 )
 
-        def hidden_product(c, first=0, last=WIDTH):
+        def hidden_product(bank, c, first, last, stop):
             part = slice(first, last)
             nc.tensor.matmul_mx(
-                out=y[c][:, part], lhsT=wb[:, 0, cols(c)].bitcast(FP8X4), lhsT_scale=wb_s[:, 0, cols(c)],
-                rhs=hid[:, part].bitcast(FP8X4), rhs_scale=hid_s[:, part], start=False, stop=(last == WIDTH),
+                out=bank[:, part], lhsT=wb[:, 0, cols(c)].bitcast(FP8X4), lhsT_scale=wb_s[:, 0, cols(c)],
+                rhs=hid[:, part].bitcast(FP8X4), rhs_scale=hid_s[:, part], start=False, stop=stop,
             )
 
-        def store(c, pieces):
-            width = WIDTH // pieces
-            for piece in range(pieces):
-                part = cols(piece, width)
-                if c % 2 == 0:
-                    nc.scalar.copy(out=result[c][:, part], in_=y[c][:, part])
-                else:
-                    nc.vector.tensor_copy(out=result[c][:, part], in_=y[c][:, part])
-                nc.sync.dma_start(out=out[cols(c), part], in_=result[c][:, part])
+        def store(copy, bank, c, first, last):
+            part = slice(first, last)
+            copy(out=result[c][:, part], in_=bank[:, part])
+            nc.sync.dma_start(out=out[cols(c), part], in_=result[c][:, part])
 
-        skip_product(0)
-        skip_product(1)
+        on_scalar, on_vector = nc.scalar.copy, nc.vector.tensor_copy
         for c in range(2):
-            hidden_product(c, 0, 2 * P)
-        for c in range(2):
-            hidden_product(c, 2 * P, 3 * P)
-        for c in range(2):
-            hidden_product(c, 3 * P, WIDTH)
-            store(c, 2)
-        skip_product(2)
-        hidden_product(2)
-        store(2, 2)
-        skip_product(3)
-        hidden_product(3)
-        store(3, 2)
+            skip_product(y[c], c)
+        for first, last in ((0, HALF), (HALF, LAST * P), (LAST * P, WIDTH)):
+            for c in range(2):
+                hidden_product(y[c], c, first, last, last == WIDTH)
+        for first in (0, HALF):
+            store(on_scalar, y[0], 0, first, first + HALF)
+            store(on_vector, y[1], 1, first, first + HALF)
+        for c, copy in ((2, on_scalar), (LAST, on_vector)):
+            skip_product(y[c], c)
+            hidden_product(y[c], c, 0, WIDTH, True)
+            for first in (0, HALF):
+                store(copy, y[c], c, first, first + HALF)

from contextlib import ExitStack

import concourse.mybir as mybir

K, L, T, R, N = 1024, 512, 512, 512, 512
FLOPS = 2 * (K * R * T + L * R * T + R * N * T + K * N * T)

F32 = mybir.dt.float32
BF16 = mybir.dt.bfloat16
I32 = mybir.dt.int32
U32 = mybir.dt.uint32
U8 = mybir.dt.uint8
FP8X4 = mybir.dt.float8_e4m3fn_x4
FP4X4 = mybir.dt.float4_e2m1fn_x4

P = 128
PACK = 4
WIDTH = 512
TILES = WIDTH // P
LAST = TILES - 1
HALF = WIDTH // 2
QUADRANT = 32
ROWS = 4
WARM_UP = 8


def cols(i, width=P):
    return slice(i * width, (i + 1) * width)


def tile_mix_conditioned_hidden_kernel(
    tc, xt_words, xt_scales, wa_words, wa_scales, cq_words, cq_scales,
    wc_words, wc_scales, wb_words, wb_scales, wy_words, wy_scales, out,
):
    nc = tc.nc
    with ExitStack() as ctx:
        keep = ctx.enter_context(tc.tile_pool(name="keep", bufs=1))
        psum = ctx.enter_context(tc.psum_pool(name="psum", bufs=1))
        ctx.enter_context(tc.manual_schedule())

        def sbuf(name, shape, dtype):
            return keep.tile(shape, dtype, name=name, align_bytes=64)

        xt = [sbuf("xt%d" % g, [P, 1, WIDTH], U32) for g in range(2)]
        cq, wb = sbuf("cq", [P, 1, WIDTH], U32), sbuf("wb", [P, 1, WIDTH], U32)
        wa, wc, wy = sbuf("wa", [P, 2, 2 * WIDTH], U8), sbuf("wc", [P, 1, 2 * WIDTH], U8), sbuf("wy", [P, 2, 2 * WIDTH], U8)
        xt_s, cq_s, wb_s = sbuf("xt_s", [P, 2, WIDTH], U8), sbuf("cq_s", [P, 1, WIDTH], U8), sbuf("wb_s", [P, 1, WIDTH], U8)
        wa_s, wc_s, wy_s = sbuf("wa_s", [P, 2, WIDTH], U8), sbuf("wc_s", [P, 1, WIDTH], U8), sbuf("wy_s", [P, 2, WIDTH], U8)

        for plane in (wa_s, xt_s, wy_s, wc_s, cq_s, wb_s):
            nc.vector.memset(plane[:].bitcast(U32), 0)

        def load_fp8(tile, words):
            nc.sync.dma_start(out=tile[:].bitcast(I32), in_=words.rearrange("z p c t -> p z (c t)").bitcast(I32))

        def load_fp4(tile, words):
            nc.sync.dma_start(out=tile[:].bitcast(I32), in_=words.rearrange("z p c -> p z c").bitcast(I32))

        def load_scale_rows(queue, plane, scales, rows):
            for r in rows:
                queue.dma_start(
                    out=plane[:].bitcast(I32)[r:P:QUADRANT, :, :],
                    in_=scales.bitcast(I32)[:, r : 4 * ROWS : ROWS, :].rearrange("z q c -> q z c"),
                )

        load_fp8(xt[0], xt_words[0:1])
        load_scale_rows(nc.sync, wa_s, wa_scales, (0, 2))
        load_scale_rows(nc.scalar, wa_s, wa_scales, (1, 3))
        load_fp4(wa, wa_words)
        load_scale_rows(nc.scalar, xt_s, xt_scales, (0, 1))
        load_scale_rows(nc.sync, xt_s, xt_scales, (2, 3))
        load_fp4(wc, wc_words)
        load_scale_rows(nc.sync, wc_s, wc_scales, (0, 1))
        load_fp8(xt[1], xt_words[1:2])
        load_scale_rows(nc.sync, wc_s, wc_scales, (2, 3))
        load_fp8(cq, cq_words)
        load_scale_rows(nc.sync, cq_s, cq_scales, range(ROWS))
        load_fp4(wy, wy_words)
        load_scale_rows(nc.gpsimd, wy_s, wy_scales, (0, 1))
        load_scale_rows(nc.sync, wy_s, wy_scales, (2, 3))
        load_fp8(wb, wb_words)
        load_scale_rows(nc.sync, wb_s, wb_scales, range(ROWS))

        def sort_scales(name, plane):
            scales = sbuf(name, [P, PACK, P], U8)
            nc.vector.tensor_copy(out=scales[:], in_=plane.rearrange("p (m j) -> p j m", j=PACK))
            return [scales[:, j, :] for j in range(PACK)]

        def sort_codes(name, words, pieces):
            by_slot = words.rearrange("p (m j b) -> p j m b", j=PACK, b=2)
            per_piece = PACK // pieces
            result = []
            for piece in range(pieces):
                codes = sbuf("%s_%d" % (name, piece), [P, per_piece * 2 * P], U8)
                nc.vector.tensor_copy(
                    out=codes[:].rearrange("p (j m b) -> p j m b", j=per_piece, b=2),
                    in_=by_slot[:, cols(piece, per_piece), :, :],
                )
                result.extend(codes[:, cols(j, 2 * P)] for j in range(per_piece))
            return result

        wa_sorted_s = [sort_scales("wa_sorted_s%d" % g, wa_s[:, g, :]) for g in range(2)]
        wa_sorted = [sort_codes("wa_sorted0", wa[:, 0, :], PACK), sort_codes("wa_sorted1", wa[:, 1, :], 1)]
        wc_sorted = sort_codes("wc_sorted", wc[:, 0, :], 1)
        wc_sorted_s = sort_scales("wc_sorted_s", wc_s[:, 0, :])

        y = [psum.tile([P, WIDTH], F32, name="y%d" % c, tag="y%d" % c) for c in range(TILES)]
        for w in range(WARM_UP):
            nc.tensor.matmul_mx(
                out=y[LAST][:, cols(0)], lhsT=xt[0][:, 0, cols(0)].bitcast(FP8X4), lhsT_scale=wa_s[:, 0, cols(0)],
                rhs=xt[0][:, 0, cols(1)].bitcast(FP8X4), rhs_scale=wa_s[:, 0, cols(1)], start=True, stop=True,
            )

        z = [psum.tile([P, PACK, P], F32, name="z%d" % i, tag="z%d" % i) for i in range(TILES)]
        grouped = [sbuf("grouped%d" % i, [P, P * PACK], BF16) for i in range(TILES)]
        hid = sbuf("hid", [P, WIDTH], U32)
        hid_s = sbuf("hid_s", [P, WIDTH], U8)

        def token_pass(i, g, j):
            nc.tensor.matmul_mx(
                out=z[i][:, j, :], lhsT=wa_sorted[g][j].bitcast(FP4X4), lhsT_scale=wa_sorted_s[g][j],
                rhs=xt[g][:, 0, cols(i)].bitcast(FP8X4), rhs_scale=xt_s[:, g, cols(i)],
                start=(g == 0 and j == 0), stop=False,
            )

        def condition_pass(i, j):
            nc.tensor.matmul_mx(
                out=z[i][:, j, :], lhsT=wc_sorted[j].bitcast(FP4X4), lhsT_scale=wc_sorted_s[j],
                rhs=cq[:, 0, cols(i)].bitcast(FP8X4), rhs_scale=cq_s[:, 0, cols(i)],
                start=False, stop=(j == PACK - 1),
            )

        def close_tile(i):
            for j in range(PACK):
                condition_pass(i, j)
            src = z[i][:].rearrange("p j t -> p t j")
            dst = grouped[i][:].rearrange("p (t j) -> p t j", j=PACK)
            if i == 1:
                nc.vector.tensor_scalar(out=dst, in0=src, scalar1=0.0, scalar2=None, op0=mybir.AluOpType.max)
            else:
                nc.scalar.activation(out=dst, in_=src, func=mybir.ActivationFunctionType.Relu)

        for j in range(PACK):
            for i in range(TILES):
                token_pass(i, 0, j)
        for i in range(LAST):
            for j in range(PACK):
                token_pass(i, 1, j)
        for i in range(LAST):
            close_tile(i)
        for j in range(PACK):
            token_pass(LAST, 1, j)
        close_tile(LAST)
        for i in range(TILES):
            nc.vector.quantize_mx(out=hid[:, cols(i)].bitcast(FP8X4), scales=hid_s[:, cols(i)], in_=grouped[i][:])

        result = [keep.tile([P, WIDTH], F32, name="result%d" % c) for c in range(TILES)]

        def skip_product(bank, c):
            for g in range(2):
                nc.tensor.matmul_mx(
                    out=bank[:], lhsT=wy[:, g, cols(c, 2 * P)].bitcast(FP4X4), lhsT_scale=wy_s[:, g, cols(c)],
                    rhs=xt[g][:, 0, :].bitcast(FP8X4), rhs_scale=xt_s[:, g, :], start=(g == 0), stop=False,
                )

        def hidden_product(bank, c, first, last, stop):
            part = slice(first, last)
            nc.tensor.matmul_mx(
                out=bank[:, part], lhsT=wb[:, 0, cols(c)].bitcast(FP8X4), lhsT_scale=wb_s[:, 0, cols(c)],
                rhs=hid[:, part].bitcast(FP8X4), rhs_scale=hid_s[:, part], start=False, stop=stop,
            )

        def store(copy, bank, c, first, last):
            part = slice(first, last)
            copy(out=result[c][:, part], in_=bank[:, part])
            nc.sync.dma_start(out=out[cols(c), part], in_=result[c][:, part])

        on_scalar, on_vector = nc.scalar.copy, nc.vector.tensor_copy
        for c in range(2):
            skip_product(y[c], c)
        for first, last in ((0, HALF), (HALF, LAST * P), (LAST * P, WIDTH)):
            for c in range(2):
                hidden_product(y[c], c, first, last, last == WIDTH)
        for first in (0, HALF):
            store(on_scalar, y[0], 0, first, first + HALF)
            store(on_vector, y[1], 1, first, first + HALF)
        for c, copy in ((2, on_scalar), (LAST, on_vector)):
            skip_product(y[c], c)
            hidden_product(y[c], c, 0, WIDTH, True)
            for first in (0, HALF):
                store(copy, y[c], c, first, first + HALF)
